import numpy as np
import ml_dtypes


def mxq(x, axis, fmt="e4m3"):
    dtype, down = {"e4m3": (ml_dtypes.float8_e4m3fn, 7), "e5m2": (ml_dtypes.float8_e5m2, 14)}[fmt]
    v = np.moveaxis(np.asarray(x, np.float32).astype(ml_dtypes.bfloat16).astype(np.float64), axis, -1)
    blocks = v.reshape(v.shape[:-1] + (-1, 32))
    amax = np.abs(blocks).max(-1, keepdims=True)
    byte = np.maximum(np.where(amax > 0, np.frexp(amax)[1] - 1 + 127, 0) - down, 1)
    scale = np.exp2(byte - 127.0)
    codes = (blocks / scale).astype(np.float32).astype(dtype).astype(np.float64)
    return np.moveaxis((codes * scale).reshape(v.shape), -1, axis)


WIDE = False


def mx_kscale(k):
    if not WIDE:
        return np.ones(k)
    levels = np.array([10, -10, 5, -5, 0])
    if k % 512:
        return np.exp2(np.random.permutation(np.resize(levels, k // 32))).repeat(32)
    a = np.empty((k // 512, 16))
    for p in range(k // 512):
        a[p, :8] = np.random.permutation(np.resize(levels, 8))
        for g in range(8):
            far = levels[np.abs(levels - a[p, g]) >= 10]
            a[p, g + 8] = far[np.random.randint(len(far))]
    return np.exp2(a.ravel()).repeat(32)


def f64(x):
    return np.asarray(x).astype(np.float64)


def striped(idx):
    return np.tile(idx.reshape(-1, 16).T, (8, 1)).astype(np.uint16)


def unstriped(offs):
    return offs[:16].T.reshape(-1).astype(np.int64)


def sigmoid(v):
    return 1.0 / (1.0 + np.exp(-np.maximum(v, -700.0)))

def planes(y):
    n, m = y.shape
    v = y.astype(np.float32).astype(ml_dtypes.bfloat16).astype(np.float64).reshape(n // 32, 32, m)
    top = np.abs(v).max(1)
    byte = np.clip(np.where(top > 0, np.frexp(top)[1] - 1 + 127 - 7, 1), 1, 254)
    codes = (v * np.exp2(127.0 - byte)[:, None, :]).reshape(n, m).astype(np.float32).astype(ml_dtypes.float8_e4m3fn).view(np.uint8)
    words = codes.reshape(n // 512, 128, 4, m).transpose(0, 1, 3, 2)
    return np.ascontiguousarray(words), np.ascontiguousarray(byte.astype(np.uint8).reshape(n // 512, 16, m))


K, T, S, N = 512, 1024, 512, 512


def setup_inputs():
    n = np.random.standard_normal
    s = mx_kscale(K)[:, None]
    return {
        "xT": (n((K, T)) * s).astype(np.float32),
        "side": n((N, T)).astype(np.float32),
        "w1": (n((K, N)) / np.sqrt(K) / s).astype(np.float32),
        "offs": striped(np.random.permutation(T)[:S]),
    }


def reference(xT, side, w1, offs):
    xq = mxq(f64(xT)[:, unstriped(offs)], 0, "e4m3")
    y = mxq(f64(w1), 0, "e4m3").T @ xq
    g = f64(side)[:, unstriped(offs)]
    out_0 = y * sigmoid(g)
    return (out_0,) + planes(out_0)

@@ -1,0 +1,108 @@
+from contextlib import ExitStack
+
+import concourse.mybir as mybir
+
+K, T, S, N = 512, 1024, 512, 512
+FLOPS = 2 * K * N * S
+
+F32 = mybir.dt.float32
+BF16 = mybir.dt.bfloat16
+I32 = mybir.dt.int32
+U32 = mybir.dt.uint32
+U16 = mybir.dt.uint16
+U8 = mybir.dt.uint8
+FP8X4 = mybir.dt.float8_e4m3fn_x4
+SIGMOID = mybir.ActivationFunctionType.Sigmoid
+MULT = mybir.AluOpType.mult
+
+P = 128
+PACK = 4
+HALF = S // 2
+
+
+def tile_picked_sidegate_sigmoid_lo_kernel(tc, xT, side, w1, offs, out_0, out_1, out_2):
+    nc = tc.nc
+    with ExitStack() as ctx:
+        keep = ctx.enter_context(tc.tile_pool(name="keep", bufs=1))
+        psum = ctx.enter_context(tc.psum_pool(name="psum", bufs=1))
+
+        offsets = keep.tile([P, S // 16], U16, name="offsets")
+        x_rows = [keep.tile([P, T], F32, name="x_rows%d" % j, align_bytes=64) for j in range(PACK)]
+        side_rows = [keep.tile([P, T], F32, name="side_rows%d" % t, align_bytes=64) for t in range(PACK)]
+        w_raw = keep.tile([P, PACK, N], F32, name="w_raw", align_bytes=64)
+
+        x_view = xT.rearrange("(p j) c -> p j c", j=PACK)
+        side_view = side.rearrange("(p t) c -> p t c", t=PACK)
+        out_view = out_0.rearrange("(p t) s -> p t s", t=PACK)
+
+        nc.sync.dma_start(x_rows[0][:], x_view[:, 0, :])
+        nc.sync.dma_start(offsets[:], offs)
+        for j in range(1, PACK):
+            nc.sync.dma_start(x_rows[j][:], x_view[:, j, :])
+        nc.sync.dma_start(w_raw[:], w1.rearrange("(p j) c -> p j c", j=PACK))
+        for t in range(PACK):
+            nc.sync.dma_start(side_rows[t][:], side_view[:, t, :])
+
+        x_picked = keep.tile([P, PACK, S], BF16, name="x_picked", align_bytes=64)
+        for j in range(PACK):
+            nc.vector.tensor_copy(x_picked[:, j, :], x_rows[j][:].indirect(offsets[:]))
+        x_grouped = keep.tile([P, S, PACK], BF16, name="x_grouped", align_bytes=64)
+        nc.vector.tensor_copy(x_grouped[:], x_picked[:].rearrange("p j s -> p s j"))
+        x_codes = keep.tile([P, S], U32, name="x_codes", align_bytes=64)
+        x_scales = keep.tile([P, S], U8, name="x_scales", align_bytes=64)
+        nc.vector.quantize_mx(out=x_codes[:].bitcast(FP8X4), scales=x_scales[:], in_=x_grouped[:].rearrange("p s j -> p (s j)"))
+
+        w_grouped = keep.tile([P, N * PACK], BF16, name="w_grouped", align_bytes=64)
+        w_out = w_grouped[:].rearrange("p (t m j) -> p m t j", t=PACK, j=PACK)
+        w_in = w_raw[:].rearrange("p j (m t) -> p m t j", t=PACK)
+        nc.scalar.copy(w_out[:, 0 : P // 2], w_in[:, 0 : P // 2])
+        nc.vector.tensor_copy(w_out[:, P // 2 : P], w_in[:, P // 2 : P])
+        w_codes = keep.tile([P, N], U32, name="w_codes", align_bytes=64)
+        w_scales = keep.tile([P, N], U8, name="w_scales", align_bytes=64)
+        nc.vector.quantize_mx(out=w_codes[:].bitcast(FP8X4), scales=w_scales[:], in_=w_grouped[:])
+
+        acc = [psum.tile([P, S], F32, name="acc%d" % t) for t in range(PACK)]
+        for t in range(PACK):
+            cols = slice(t * P, (t + 1) * P)
+            nc.tensor.matmul_mx(
+                out=acc[t][:],
+                lhsT=w_codes[:, cols].bitcast(FP8X4),
+                lhsT_scale=w_scales[:, cols],
+                rhs=x_codes[:].bitcast(FP8X4),
+                rhs_scale=x_scales[:],
+                start=True,
+                stop=True,
+            )
+
+        gate = keep.tile([P, PACK, S], F32, name="gate", align_bytes=64)
+        y = keep.tile([P, PACK, S], F32, name="y", align_bytes=64)
+        y_grouped = keep.tile([P, S, PACK], BF16, name="y_grouped", align_bytes=64)
+        y_codes = keep.tile([P, S], U32, name="y_codes", align_bytes=64)
+        y_scales = keep.tile([P, S], U8, name="y_scales", align_bytes=64)
+
+        last = PACK - 1
+        for t in range(last):
+            nc.scalar.activation(gate[:, t, :], side_rows[t][:].indirect(offsets[:]), SIGMOID)
+            nc.vector.tensor_tensor(y[:, t, :], acc[t][:], gate[:, t, :], MULT)
+            nc.sync.dma_start(out_view[:, t, :], y[:, t, :])
+
+        halves = [slice(0, HALF), slice(HALF, S)]
+        for h, cols in enumerate(halves):
+            piece = offsets[:, h * HALF // 16 : (h + 1) * HALF // 16]
+            nc.scalar.activation(gate[:, last, cols], side_rows[last][:].indirect(piece), SIGMOID)
+        words_view = out_1[0].rearrange("p s r -> p (s r)").bitcast(I32)
+        for cols in halves:
+            nc.vector.tensor_tensor(y[:, last, cols], acc[last][:, cols], gate[:, last, cols], MULT)
+            nc.vector.tensor_copy(y_grouped[:, cols, :], y[:, :, cols].rearrange("p t s -> p s t"))
+        nc.sync.dma_start(out_view[:, last, :], y[:, last, :])
+        for cols in halves:
+            nc.vector.quantize_mx(
+                out=y_codes[:, cols].bitcast(FP8X4),
+                scales=y_scales[:, cols],
+                in_=y_grouped[:, cols, :].rearrange("p s t -> p (s t)"),
+            )
+            nc.sync.dma_start(words_view[:, cols], y_codes[:, cols].bitcast(I32))
+        scales_view = out_2[0].bitcast(I32)
+        for q in range(4):
+            queue = nc.scalar if q % 2 else nc.sync
+            queue.dma_start(scales_view[4 * q : 4 * q + 4, :], y_scales[32 * q : 32 * q + 4, :].bitcast(I32))

@@ -13,11 +13,14 @@ U16 = mybir.dt.uint16
 U8 = mybir.dt.uint8
 FP8X4 = mybir.dt.float8_e4m3fn_x4
 SIGMOID = mybir.ActivationFunctionType.Sigmoid
+COPY = mybir.ActivationFunctionType.Copy
 MULT = mybir.AluOpType.mult
 
 P = 128
 PACK = 4
 HALF = S // 2
+X_VECTOR = 352
+ROUND_VECTOR = (128, 160)
 
 
 def tile_picked_sidegate_sigmoid_lo_kernel(tc, xT, side, w1, offs, out_0, out_1, out_2):
@@ -37,17 +40,24 @@ def tile_picked_sidegate_sigmoid_lo_kernel(tc, xT, side, w1, offs, out_0, out_1,
 
         nc.sync.dma_start(x_rows[0][:], x_view[:, 0, :])
         nc.sync.dma_start(offsets[:], offs)
+        nc.sync.dma_start(side_rows[0][:], side_view[:, 0, :])
         for j in range(1, PACK):
             nc.sync.dma_start(x_rows[j][:], x_view[:, j, :])
         nc.sync.dma_start(w_raw[:], w1.rearrange("(p j) c -> p j c", j=PACK))
-        for t in range(PACK):
+        for t in range(1, PACK):
             nc.sync.dma_start(side_rows[t][:], side_view[:, t, :])
 
         x_picked = keep.tile([P, PACK, S], BF16, name="x_picked", align_bytes=64)
-        for j in range(PACK):
+        gate = keep.tile([P, PACK, S], F32, name="gate", align_bytes=64)
+        nc.scalar.activation(gate[:, 0, :], side_rows[0][:].indirect(offsets[:]), SIGMOID)
+        last = PACK - 1
+        for j in range(last):
             nc.vector.tensor_copy(x_picked[:, j, :], x_rows[j][:].indirect(offsets[:]))
+        nc.vector.tensor_copy(x_picked[:, last, 0:HALF], x_rows[last][:].indirect(offsets[:, 0 : HALF // 16]))
+        nc.scalar.activation(x_picked[:, last, HALF:S], x_rows[last][:].indirect(offsets[:, HALF // 16 : S // 16]), COPY)
         x_grouped = keep.tile([P, S, PACK], BF16, name="x_grouped", align_bytes=64)
-        nc.vector.tensor_copy(x_grouped[:], x_picked[:].rearrange("p j s -> p s j"))
+        nc.vector.tensor_copy(x_grouped[:, 0:X_VECTOR], x_picked[:, :, 0:X_VECTOR].rearrange("p j s -> p s j"))
+        nc.scalar.copy(x_grouped[:, X_VECTOR:S], x_picked[:, :, X_VECTOR:S].rearrange("p j s -> p s j"))
         x_codes = keep.tile([P, S], U32, name="x_codes", align_bytes=64)
         x_scales = keep.tile([P, S], U8, name="x_scales", align_bytes=64)
         nc.vector.quantize_mx(out=x_codes[:].bitcast(FP8X4), scales=x_scales[:], in_=x_grouped[:].rearrange("p s j -> p (s j)"))
@@ -55,15 +65,22 @@ def tile_picked_sidegate_sigmoid_lo_kernel(tc, xT, side, w1, offs, out_0, out_1,
         w_grouped = keep.tile([P, N * PACK], BF16, name="w_grouped", align_bytes=64)
         w_out = w_grouped[:].rearrange("p (t m j) -> p m t j", t=PACK, j=PACK)
         w_in = w_raw[:].rearrange("p j (m t) -> p m t j", t=PACK)
-        nc.scalar.copy(w_out[:, 0 : P // 2], w_in[:, 0 : P // 2])
-        nc.vector.tensor_copy(w_out[:, P // 2 : P], w_in[:, P // 2 : P])
+        nc.vector.tensor_copy(w_out[:, :, 0:2], w_in[:, :, 0:2])
+        nc.scalar.copy(w_out[:, :, last], w_in[:, :, last])
+        nc.vector.tensor_copy(w_out[:, :, 2], w_in[:, :, 2])
         w_codes = keep.tile([P, N], U32, name="w_codes", align_bytes=64)
         w_scales = keep.tile([P, N], U8, name="w_scales", align_bytes=64)
-        nc.vector.quantize_mx(out=w_codes[:].bitcast(FP8X4), scales=w_scales[:], in_=w_grouped[:])
 
         acc = [psum.tile([P, S], F32, name="acc%d" % t) for t in range(PACK)]
         for t in range(PACK):
             cols = slice(t * P, (t + 1) * P)
+            if t % 2 == 0:
+                pair = slice(t * P, (t + 2) * P)
+                nc.vector.quantize_mx(
+                    out=w_codes[:, pair].bitcast(FP8X4),
+                    scales=w_scales[:, pair],
+                    in_=w_grouped[:, t * N : (t + 2) * N],
+                )
             nc.tensor.matmul_mx(
                 out=acc[t][:],
                 lhsT=w_codes[:, cols].bitcast(FP8X4),
@@ -74,15 +91,14 @@ def tile_picked_sidegate_sigmoid_lo_kernel(tc, xT, side, w1, offs, out_0, out_1,
                 stop=True,
             )
 
-        gate = keep.tile([P, PACK, S], F32, name="gate", align_bytes=64)
         y = keep.tile([P, PACK, S], F32, name="y", align_bytes=64)
         y_grouped = keep.tile([P, S, PACK], BF16, name="y_grouped", align_bytes=64)
         y_codes = keep.tile([P, S], U32, name="y_codes", align_bytes=64)
         y_scales = keep.tile([P, S], U8, name="y_scales", align_bytes=64)
 
-        last = PACK - 1
         for t in range(last):
-            nc.scalar.activation(gate[:, t, :], side_rows[t][:].indirect(offsets[:]), SIGMOID)
+            if t > 0:
+                nc.scalar.activation(gate[:, t, :], side_rows[t][:].indirect(offsets[:]), SIGMOID)
             nc.vector.tensor_tensor(y[:, t, :], acc[t][:], gate[:, t, :], MULT)
             nc.sync.dma_start(out_view[:, t, :], y[:, t, :])
 
@@ -91,9 +107,12 @@ def tile_picked_sidegate_sigmoid_lo_kernel(tc, xT, side, w1, offs, out_0, out_1,
             piece = offsets[:, h * HALF // 16 : (h + 1) * HALF // 16]
             nc.scalar.activation(gate[:, last, cols], side_rows[last][:].indirect(piece), SIGMOID)
         words_view = out_1[0].rearrange("p s r -> p (s r)").bitcast(I32)
-        for cols in halves:
+        for cols, share in zip(halves, ROUND_VECTOR):
             nc.vector.tensor_tensor(y[:, last, cols], acc[last][:, cols], gate[:, last, cols], MULT)
-            nc.vector.tensor_copy(y_grouped[:, cols, :], y[:, :, cols].rearrange("p t s -> p s t"))
+            first = slice(cols.start, cols.start + share)
+            rest = slice(cols.start + share, cols.stop)
+            nc.vector.tensor_copy(y_grouped[:, first, :], y[:, :, first].rearrange("p t s -> p s t"))
+            nc.scalar.copy(y_grouped[:, rest, :], y[:, :, rest].rearrange("p t s -> p s t"))
         nc.sync.dma_start(out_view[:, last, :], y[:, last, :])
         for cols in halves:
             nc.vector.quantize_mx(

@@ -19,8 +19,7 @@ MULT = mybir.AluOpType.mult
 P = 128
 PACK = 4
 HALF = S // 2
-X_VECTOR = 352
-ROUND_VECTOR = (128, 160)
+X_VECTOR = 416
 
 
 def tile_picked_sidegate_sigmoid_lo_kernel(tc, xT, side, w1, offs, out_0, out_1, out_2):
@@ -40,34 +39,38 @@ def tile_picked_sidegate_sigmoid_lo_kernel(tc, xT, side, w1, offs, out_0, out_1,
 
         nc.sync.dma_start(x_rows[0][:], x_view[:, 0, :])
         nc.sync.dma_start(offsets[:], offs)
-        nc.sync.dma_start(side_rows[0][:], side_view[:, 0, :])
         for j in range(1, PACK):
             nc.sync.dma_start(x_rows[j][:], x_view[:, j, :])
         nc.sync.dma_start(w_raw[:], w1.rearrange("(p j) c -> p j c", j=PACK))
-        for t in range(1, PACK):
+        for t in range(PACK):
             nc.sync.dma_start(side_rows[t][:], side_view[:, t, :])
 
         x_picked = keep.tile([P, PACK, S], BF16, name="x_picked", align_bytes=64)
         gate = keep.tile([P, PACK, S], F32, name="gate", align_bytes=64)
-        nc.scalar.activation(gate[:, 0, :], side_rows[0][:].indirect(offsets[:]), SIGMOID)
         last = PACK - 1
-        for j in range(last):
-            nc.vector.tensor_copy(x_picked[:, j, :], x_rows[j][:].indirect(offsets[:]))
+        nc.scalar.activation(x_picked[:, 0, :], x_rows[0][:].indirect(offsets[:]), COPY)
+        nc.vector.tensor_copy(x_picked[:, 1, :], x_rows[1][:].indirect(offsets[:]))
+        nc.vector.tensor_copy(x_picked[:, 2, :], x_rows[2][:].indirect(offsets[:]))
         nc.vector.tensor_copy(x_picked[:, last, 0:HALF], x_rows[last][:].indirect(offsets[:, 0 : HALF // 16]))
         nc.scalar.activation(x_picked[:, last, HALF:S], x_rows[last][:].indirect(offsets[:, HALF // 16 : S // 16]), COPY)
         x_grouped = keep.tile([P, S, PACK], BF16, name="x_grouped", align_bytes=64)
-        nc.vector.tensor_copy(x_grouped[:, 0:X_VECTOR], x_picked[:, :, 0:X_VECTOR].rearrange("p j s -> p s j"))
+        nc.vector.tensor_copy(x_grouped[:, 0:HALF], x_picked[:, :, 0:HALF].rearrange("p j s -> p s j"))
+        nc.vector.tensor_copy(x_grouped[:, HALF:X_VECTOR], x_picked[:, :, HALF:X_VECTOR].rearrange("p j s -> p s j"))
         nc.scalar.copy(x_grouped[:, X_VECTOR:S], x_picked[:, :, X_VECTOR:S].rearrange("p j s -> p s j"))
         x_codes = keep.tile([P, S], U32, name="x_codes", align_bytes=64)
         x_scales = keep.tile([P, S], U8, name="x_scales", align_bytes=64)
-        nc.vector.quantize_mx(out=x_codes[:].bitcast(FP8X4), scales=x_scales[:], in_=x_grouped[:].rearrange("p s j -> p (s j)"))
+        halves = [slice(0, HALF), slice(HALF, S)]
+        for cols in halves:
+            nc.vector.quantize_mx(
+                out=x_codes[:, cols].bitcast(FP8X4),
+                scales=x_scales[:, cols],
+                in_=x_grouped[:, cols, :].rearrange("p s j -> p (s j)"),
+            )
 
         w_grouped = keep.tile([P, N * PACK], BF16, name="w_grouped", align_bytes=64)
         w_out = w_grouped[:].rearrange("p (t m j) -> p m t j", t=PACK, j=PACK)
         w_in = w_raw[:].rearrange("p j (m t) -> p m t j", t=PACK)
-        nc.vector.tensor_copy(w_out[:, :, 0:2], w_in[:, :, 0:2])
-        nc.scalar.copy(w_out[:, :, last], w_in[:, :, last])
-        nc.vector.tensor_copy(w_out[:, :, 2], w_in[:, :, 2])
+        nc.vector.tensor_copy(w_out, w_in)
         w_codes = keep.tile([P, N], U32, name="w_codes", align_bytes=64)
         w_scales = keep.tile([P, N], U8, name="w_scales", align_bytes=64)
 
@@ -97,22 +100,30 @@ def tile_picked_sidegate_sigmoid_lo_kernel(tc, xT, side, w1, offs, out_0, out_1,
         y_scales = keep.tile([P, S], U8, name="y_scales", align_bytes=64)
 
         for t in range(last):
-            if t > 0:
-                nc.scalar.activation(gate[:, t, :], side_rows[t][:].indirect(offsets[:]), SIGMOID)
+            nc.scalar.activation(gate[:, t, :], side_rows[t][:].indirect(offsets[:]), SIGMOID)
             nc.vector.tensor_tensor(y[:, t, :], acc[t][:], gate[:, t, :], MULT)
             nc.sync.dma_start(out_view[:, t, :], y[:, t, :])
 
-        halves = [slice(0, HALF), slice(HALF, S)]
-        for h, cols in enumerate(halves):
-            piece = offsets[:, h * HALF // 16 : (h + 1) * HALF // 16]
+        pieces = [slice(0, 256), slice(256, 384), slice(384, 512)]
+        for cols in pieces:
+            piece = offsets[:, cols.start // 16 : cols.stop // 16]
             nc.scalar.activation(gate[:, last, cols], side_rows[last][:].indirect(piece), SIGMOID)
         words_view = out_1[0].rearrange("p s r -> p (s r)").bitcast(I32)
-        for cols, share in zip(halves, ROUND_VECTOR):
+
+        def multiply(cols):
             nc.vector.tensor_tensor(y[:, last, cols], acc[last][:, cols], gate[:, last, cols], MULT)
-            first = slice(cols.start, cols.start + share)
-            rest = slice(cols.start + share, cols.stop)
-            nc.vector.tensor_copy(y_grouped[:, first, :], y[:, :, first].rearrange("p t s -> p s t"))
-            nc.scalar.copy(y_grouped[:, rest, :], y[:, :, rest].rearrange("p t s -> p s t"))
+
+        def round_on(copy, start, stop):
+            copy(y_grouped[:, start:stop, :], y[:, :, start:stop].rearrange("p t s -> p s t"))
+
+        multiply(pieces[0])
+        multiply(pieces[1])
+        round_on(nc.vector.tensor_copy, 0, 128)
+        round_on(nc.scalar.copy, 128, 256)
+        multiply(pieces[2])
+        round_on(nc.vector.tensor_copy, 256, 384)
+        round_on(nc.vector.tensor_copy, 384, 448)
+        round_on(nc.scalar.copy, 448, 512)
         nc.sync.dma_start(out_view[:, last, :], y[:, last, :])
         for cols in halves:
             nc.vector.quantize_mx(

@@ -22,6 +22,13 @@ HALF = S // 2
 X_VECTOR = 416
 
 
+def interleave(copy, grouped, planes, start, stop):
+    copy(
+        grouped[:, start:stop, :].rearrange("p (c i) t -> p c t i", i=4),
+        planes[:, :, start:stop].rearrange("p t (c i) -> p c t i", i=4),
+    )
+
+
 def tile_picked_sidegate_sigmoid_lo_kernel(tc, xT, side, w1, offs, out_0, out_1, out_2):
     nc = tc.nc
     with ExitStack() as ctx:
@@ -54,9 +61,9 @@ def tile_picked_sidegate_sigmoid_lo_kernel(tc, xT, side, w1, offs, out_0, out_1,
         nc.vector.tensor_copy(x_picked[:, last, 0:HALF], x_rows[last][:].indirect(offsets[:, 0 : HALF // 16]))
         nc.scalar.activation(x_picked[:, last, HALF:S], x_rows[last][:].indirect(offsets[:, HALF // 16 : S // 16]), COPY)
         x_grouped = keep.tile([P, S, PACK], BF16, name="x_grouped", align_bytes=64)
-        nc.vector.tensor_copy(x_grouped[:, 0:HALF], x_picked[:, :, 0:HALF].rearrange("p j s -> p s j"))
-        nc.vector.tensor_copy(x_grouped[:, HALF:X_VECTOR], x_picked[:, :, HALF:X_VECTOR].rearrange("p j s -> p s j"))
-        nc.scalar.copy(x_grouped[:, X_VECTOR:S], x_picked[:, :, X_VECTOR:S].rearrange("p j s -> p s j"))
+        interleave(nc.vector.tensor_copy, x_grouped, x_picked, 0, HALF)
+        interleave(nc.vector.tensor_copy, x_grouped, x_picked, HALF, X_VECTOR)
+        interleave(nc.scalar.copy, x_grouped, x_picked, X_VECTOR, S)
         x_codes = keep.tile([P, S], U32, name="x_codes", align_bytes=64)
         x_scales = keep.tile([P, S], U8, name="x_scales", align_bytes=64)
         halves = [slice(0, HALF), slice(HALF, S)]
@@ -100,11 +107,13 @@ def tile_picked_sidegate_sigmoid_lo_kernel(tc, xT, side, w1, offs, out_0, out_1,
         y_scales = keep.tile([P, S], U8, name="y_scales", align_bytes=64)
 
         for t in range(last):
-            nc.scalar.activation(gate[:, t, :], side_rows[t][:].indirect(offsets[:]), SIGMOID)
-            nc.vector.tensor_tensor(y[:, t, :], acc[t][:], gate[:, t, :], MULT)
+            for cols in halves if t == last - 1 else [slice(0, S)]:
+                piece = offsets[:, cols.start // 16 : cols.stop // 16]
+                nc.scalar.activation(gate[:, t, cols], side_rows[t][:].indirect(piece), SIGMOID)
+                nc.vector.tensor_tensor(y[:, t, cols], acc[t][:, cols], gate[:, t, cols], MULT)
             nc.sync.dma_start(out_view[:, t, :], y[:, t, :])
 
-        pieces = [slice(0, 256), slice(256, 384), slice(384, 512)]
+        pieces = [slice(0, 128), slice(128, 256), slice(256, 384), slice(384, 512)]
         for cols in pieces:
             piece = offsets[:, cols.start // 16 : cols.stop // 16]
             nc.scalar.activation(gate[:, last, cols], side_rows[last][:].indirect(piece), SIGMOID)
@@ -114,13 +123,14 @@ def tile_picked_sidegate_sigmoid_lo_kernel(tc, xT, side, w1, offs, out_0, out_1,
             nc.vector.tensor_tensor(y[:, last, cols], acc[last][:, cols], gate[:, last, cols], MULT)
 
         def round_on(copy, start, stop):
-            copy(y_grouped[:, start:stop, :], y[:, :, start:stop].rearrange("p t s -> p s t"))
+            interleave(copy, y_grouped, y, start, stop)
 
         multiply(pieces[0])
         multiply(pieces[1])
         round_on(nc.vector.tensor_copy, 0, 128)
-        round_on(nc.scalar.copy, 128, 256)
         multiply(pieces[2])
+        round_on(nc.scalar.copy, 128, 256)
+        multiply(pieces[3])
         round_on(nc.vector.tensor_copy, 256, 384)
         round_on(nc.vector.tensor_copy, 384, 448)
         round_on(nc.scalar.copy, 448, 512)

from contextlib import ExitStack

import concourse.mybir as mybir

K, T, S, N = 512, 1024, 512, 512
FLOPS = 2 * K * N * S

F32 = mybir.dt.float32
BF16 = mybir.dt.bfloat16
I32 = mybir.dt.int32
U32 = mybir.dt.uint32
U16 = mybir.dt.uint16
U8 = mybir.dt.uint8
FP8X4 = mybir.dt.float8_e4m3fn_x4
SIGMOID = mybir.ActivationFunctionType.Sigmoid
COPY = mybir.ActivationFunctionType.Copy
MULT = mybir.AluOpType.mult

P = 128
PACK = 4
HALF = S // 2
X_VECTOR = 416


def interleave(copy, grouped, planes, start, stop):
    copy(
        grouped[:, start:stop, :].rearrange("p (c i) t -> p c t i", i=4),
        planes[:, :, start:stop].rearrange("p t (c i) -> p c t i", i=4),
    )


def tile_picked_sidegate_sigmoid_lo_kernel(tc, xT, side, w1, offs, out_0, out_1, out_2):
    nc = tc.nc
    with ExitStack() as ctx:
        keep = ctx.enter_context(tc.tile_pool(name="keep", bufs=1))
        psum = ctx.enter_context(tc.psum_pool(name="psum", bufs=1))

        offsets = keep.tile([P, S // 16], U16, name="offsets")
        x_rows = [keep.tile([P, T], F32, name="x_rows%d" % j, align_bytes=64) for j in range(PACK)]
        side_rows = [keep.tile([P, T], F32, name="side_rows%d" % t, align_bytes=64) for t in range(PACK)]
        w_raw = keep.tile([P, PACK, N], F32, name="w_raw", align_bytes=64)

        x_view = xT.rearrange("(p j) c -> p j c", j=PACK)
        side_view = side.rearrange("(p t) c -> p t c", t=PACK)
        out_view = out_0.rearrange("(p t) s -> p t s", t=PACK)

        nc.sync.dma_start(x_rows[0][:], x_view[:, 0, :])
        nc.sync.dma_start(offsets[:], offs)
        for j in range(1, PACK):
            nc.sync.dma_start(x_rows[j][:], x_view[:, j, :])
        nc.sync.dma_start(w_raw[:], w1.rearrange("(p j) c -> p j c", j=PACK))
        for t in range(PACK):
            nc.sync.dma_start(side_rows[t][:], side_view[:, t, :])

        x_picked = keep.tile([P, PACK, S], BF16, name="x_picked", align_bytes=64)
        gate = keep.tile([P, PACK, S], F32, name="gate", align_bytes=64)
        last = PACK - 1
        nc.scalar.activation(x_picked[:, 0, :], x_rows[0][:].indirect(offsets[:]), COPY)
        nc.vector.tensor_copy(x_picked[:, 1, :], x_rows[1][:].indirect(offsets[:]))
        nc.vector.tensor_copy(x_picked[:, 2, :], x_rows[2][:].indirect(offsets[:]))
        nc.vector.tensor_copy(x_picked[:, last, 0:HALF], x_rows[last][:].indirect(offsets[:, 0 : HALF // 16]))
        nc.scalar.activation(x_picked[:, last, HALF:S], x_rows[last][:].indirect(offsets[:, HALF // 16 : S // 16]), COPY)
        x_grouped = keep.tile([P, S, PACK], BF16, name="x_grouped", align_bytes=64)
        interleave(nc.vector.tensor_copy, x_grouped, x_picked, 0, HALF)
        interleave(nc.vector.tensor_copy, x_grouped, x_picked, HALF, X_VECTOR)
        interleave(nc.scalar.copy, x_grouped, x_picked, X_VECTOR, S)
        x_codes = keep.tile([P, S], U32, name="x_codes", align_bytes=64)
        x_scales = keep.tile([P, S], U8, name="x_scales", align_bytes=64)
        halves = [slice(0, HALF), slice(HALF, S)]
        for cols in halves:
            nc.vector.quantize_mx(
                out=x_codes[:, cols].bitcast(FP8X4),
                scales=x_scales[:, cols],
                in_=x_grouped[:, cols, :].rearrange("p s j -> p (s j)"),
            )

        w_grouped = keep.tile([P, N * PACK], BF16, name="w_grouped", align_bytes=64)
        w_out = w_grouped[:].rearrange("p (t m j) -> p m t j", t=PACK, j=PACK)
        w_in = w_raw[:].rearrange("p j (m t) -> p m t j", t=PACK)
        nc.vector.tensor_copy(w_out, w_in)
        w_codes = keep.tile([P, N], U32, name="w_codes", align_bytes=64)
        w_scales = keep.tile([P, N], U8, name="w_scales", align_bytes=64)

        acc = [psum.tile([P, S], F32, name="acc%d" % t) for t in range(PACK)]
        for t in range(PACK):
            cols = slice(t * P, (t + 1) * P)
            if t % 2 == 0:
                pair = slice(t * P, (t + 2) * P)
                nc.vector.quantize_mx(
                    out=w_codes[:, pair].bitcast(FP8X4),
                    scales=w_scales[:, pair],
                    in_=w_grouped[:, t * N : (t + 2) * N],
                )
            nc.tensor.matmul_mx(
                out=acc[t][:],
                lhsT=w_codes[:, cols].bitcast(FP8X4),
                lhsT_scale=w_scales[:, cols],
                rhs=x_codes[:].bitcast(FP8X4),
                rhs_scale=x_scales[:],
                start=True,
                stop=True,
            )

        y = keep.tile([P, PACK, S], F32, name="y", align_bytes=64)
        y_grouped = keep.tile([P, S, PACK], BF16, name="y_grouped", align_bytes=64)
        y_codes = keep.tile([P, S], U32, name="y_codes", align_bytes=64)
        y_scales = keep.tile([P, S], U8, name="y_scales", align_bytes=64)

        for t in range(last):
            for cols in halves if t == last - 1 else [slice(0, S)]:
                piece = offsets[:, cols.start // 16 : cols.stop // 16]
                nc.scalar.activation(gate[:, t, cols], side_rows[t][:].indirect(piece), SIGMOID)
                nc.vector.tensor_tensor(y[:, t, cols], acc[t][:, cols], gate[:, t, cols], MULT)
            nc.sync.dma_start(out_view[:, t, :], y[:, t, :])

        pieces = [slice(0, 128), slice(128, 256), slice(256, 384), slice(384, 512)]
        for cols in pieces:
            piece = offsets[:, cols.start // 16 : cols.stop // 16]
            nc.scalar.activation(gate[:, last, cols], side_rows[last][:].indirect(piece), SIGMOID)
        words_view = out_1[0].rearrange("p s r -> p (s r)").bitcast(I32)

        def multiply(cols):
            nc.vector.tensor_tensor(y[:, last, cols], acc[last][:, cols], gate[:, last, cols], MULT)

        def round_on(copy, start, stop):
            interleave(copy, y_grouped, y, start, stop)

        multiply(pieces[0])
        multiply(pieces[1])
        round_on(nc.vector.tensor_copy, 0, 128)
        multiply(pieces[2])
        round_on(nc.scalar.copy, 128, 256)
        multiply(pieces[3])
        round_on(nc.vector.tensor_copy, 256, 384)
        round_on(nc.vector.tensor_copy, 384, 448)
        round_on(nc.scalar.copy, 448, 512)
        nc.sync.dma_start(out_view[:, last, :], y[:, last, :])
        for cols in halves:
            nc.vector.quantize_mx(
                out=y_codes[:, cols].bitcast(FP8X4),
                scales=y_scales[:, cols],
                in_=y_grouped[:, cols, :].rearrange("p s t -> p (s t)"),
            )
            nc.sync.dma_start(words_view[:, cols], y_codes[:, cols].bitcast(I32))
        scales_view = out_2[0].bitcast(I32)
        for q in range(4):
            queue = nc.scalar if q % 2 else nc.sync
            queue.dma_start(scales_view[4 * q : 4 * q + 4, :], y_scales[32 * q : 32 * q + 4, :].bitcast(I32))
